import numpy as np
import ml_dtypes


def mxq(x, axis, fmt="e4m3"):
    dtype, down = {"e4m3": (ml_dtypes.float8_e4m3fn, 7), "e5m2": (ml_dtypes.float8_e5m2, 14)}[fmt]
    v = np.moveaxis(np.asarray(x, np.float32).astype(ml_dtypes.bfloat16).astype(np.float64), axis, -1)
    blocks = v.reshape(v.shape[:-1] + (-1, 32))
    amax = np.abs(blocks).max(-1, keepdims=True)
    byte = np.maximum(np.where(amax > 0, np.frexp(amax)[1] - 1 + 127, 0) - down, 1)
    scale = np.exp2(byte - 127.0)
    codes = (blocks / scale).astype(np.float32).astype(dtype).astype(np.float64)
    return np.moveaxis((codes * scale).reshape(v.shape), -1, axis)


WIDE = False


def mx_kscale(k):
    if not WIDE:
        return np.ones(k)
    levels = np.array([10, -10, 5, -5, 0])
    if k % 512:
        return np.exp2(np.random.permutation(np.resize(levels, k // 32))).repeat(32)
    a = np.empty((k // 512, 16))
    for p in range(k // 512):
        a[p, :8] = np.random.permutation(np.resize(levels, 8))
        for g in range(8):
            far = levels[np.abs(levels - a[p, g]) >= 10]
            a[p, g + 8] = far[np.random.randint(len(far))]
    return np.exp2(a.ravel()).repeat(32)


def f64(x):
    return np.asarray(x).astype(np.float64)


def striped(idx):
    return np.tile(idx.reshape(-1, 16).T, (8, 1)).astype(np.uint16)


def unstriped(offs):
    return offs[:16].T.reshape(-1).astype(np.int64)


def striped8(idx):
    return np.concatenate([x.reshape(-1, 16).T for x in idx]).astype(np.uint16)


def runs(offs, k):
    lists = np.stack([offs[16 * r : 16 * r + 16].T.reshape(-1) for r in range(8)]).astype(np.int64)
    return lists[np.arange(k) % 512 // 64]


def pack_weight(w):
    k, n = w.shape
    w = f64(np.asarray(w, np.float32).astype(ml_dtypes.bfloat16)).reshape(k // 32, 32, n)
    amax = np.abs(w).max(1)
    byte = np.clip(np.where(amax > 0, np.frexp(amax)[1] - 1 + 127 - 7, 1), 1, 254)
    scaled = (w * np.exp2(127.0 - byte)[:, None, :]).reshape(k, n).astype(np.float32)
    words = np.ascontiguousarray(scaled.reshape(k // 512, 128, 4, n).transpose(0, 1, 3, 2)).astype(ml_dtypes.float8_e4m3fn).view(np.uint8)
    return words, np.ascontiguousarray(byte.astype(np.uint8).reshape(k // 512, 16, n))


def unpack_weight(words, scales):
    g, p, n, _ = words.shape
    vals = np.ascontiguousarray(words).view(ml_dtypes.float8_e4m3fn).astype(np.float64) * np.repeat(np.exp2(scales.astype(np.float64) - 127.0), 8, axis=1)[..., None]
    return vals.transpose(0, 1, 3, 2).reshape(g * 512, n)


E2M1 = np.array([0.0, 0.5, 1.0, 1.5, 2.0, 3.0, 4.0, 6.0, -0.0, -0.5, -1.0, -1.5, -2.0, -3.0, -4.0, -6.0])


def pack_fp4(w):
    k, n = w.shape
    w = f64(np.asarray(w, np.float32).astype(ml_dtypes.bfloat16)).reshape(k // 32, 32, n)
    amax = np.abs(w).max(1)
    mant, ex = np.frexp(amax / 6.0)
    byte = np.clip(np.where(amax > 0, np.where(mant > 0.5, ex, ex - 1) + 127, 1), 1, 254)
    scaled = (w * np.exp2(127.0 - byte)[:, None, :]).reshape(k, n).astype(np.float32)
    c = np.ascontiguousarray(scaled.reshape(k // 512, 128, 4, n).transpose(0, 1, 3, 2)).astype(ml_dtypes.float4_e2m1fn).view(np.uint8) & 0xF
    words = (c[..., 0::2] | (c[..., 1::2] << 4)).reshape(k // 512, 128, 2 * n)
    return np.ascontiguousarray(words), np.ascontiguousarray(byte.astype(np.uint8).reshape(k // 512, 16, n))


def unpack_fp4(words, scales):
    g, _, n = scales.shape
    words = np.ascontiguousarray(words).reshape(g, 128, n, 2)
    nib = np.empty((g, 128, n, 4), np.uint8)
    nib[..., 0::2] = words & 0xF
    nib[..., 1::2] = words >> 4
    vals = E2M1[nib] * np.repeat(np.exp2(scales.astype(np.float64) - 127.0), 8, axis=1)[..., None]
    return vals.transpose(0, 1, 3, 2).reshape(g * 512, n)


def planes(y):
    n, m = y.shape
    v = y.astype(np.float32).astype(ml_dtypes.bfloat16).astype(np.float64).reshape(n // 32, 32, m)
    top = np.abs(v).max(1)
    byte = np.clip(np.where(top > 0, np.frexp(top)[1] - 1 + 127 - 7, 1), 1, 254)
    codes = (v * np.exp2(127.0 - byte)[:, None, :]).reshape(n, m).astype(np.float32).astype(ml_dtypes.float8_e4m3fn).view(np.uint8)
    words = codes.reshape(n // 512, 128, 4, m).transpose(0, 1, 3, 2)
    return np.ascontiguousarray(words), np.ascontiguousarray(byte.astype(np.uint8).reshape(n // 512, 16, m))


K, T, S, H, C = 512, 2048, 512, 512, 512


def setup_inputs():
    n = np.random.standard_normal
    s = mx_kscale(K)[:, None]
    packed_xT = pack_weight(n((K, T)) * s)
    packed_w1 = pack_fp4(n((K, H)) / np.sqrt(K) / s)
    return {
        "x_words": packed_xT[0],
        "x_scales": packed_xT[1],
        "w1_words": packed_w1[0],
        "w1_scales": packed_w1[1],
        "gs": (np.random.uniform(0.5, 1.5, (K, 1)) / s).astype(np.float32),
        "offs": striped(np.random.permutation(T)[:S]),
        "n1": striped8(np.stack([np.random.permutation(S) for _ in range(8)])),
        "n2": striped8(np.stack([np.random.permutation(S) for _ in range(8)])),
        "ca": striped(np.random.permutation(T)[:C]),
        "cb": striped(np.random.permutation(T)[:C]),
        "n3": striped8(np.stack([np.random.permutation(S) for _ in range(8)])),
        "n4": striped8(np.stack([np.random.permutation(S) for _ in range(8)])),
    }


def reference(x_words, x_scales, w1_words, w1_scales, gs, offs, n1, n2, ca, cb, n3, n4):
    x_ca = unpack_weight(x_words, x_scales)[:, unstriped(ca)]
    xq = unpack_weight(x_words, x_scales)[:, unstriped(offs)]
    y = unpack_fp4(w1_words, w1_scales).T @ xq
    z = f64(gs) * (y * (y[np.arange(H)[:, None], runs(n1, H)] - (y[np.arange(H)[:, None], runs(n2, H)])))
    zq = mxq(z, 0, "e4m3")
    a = 0.0625 * (x_ca.T @ zq)
    x_cb = unpack_weight(x_words, x_scales)[:, unstriped(cb)]
    b = 0.0625 * (x_cb.T @ zq)
    out_0 = (a - (a[np.arange(C)[:, None], runs(n3, C)])) / (np.abs(b) + np.abs(b[np.arange(C)[:, None], runs(n4, C)]) + 0.5)
    return (out_0,) + planes(out_0)

@@ -1,0 +1,223 @@
+from contextlib import ExitStack
+
+import concourse.mybir as mybir
+
+F32 = mybir.dt.float32
+BF16 = mybir.dt.bfloat16
+I32 = mybir.dt.int32
+U32 = mybir.dt.uint32
+U16 = mybir.dt.uint16
+U8 = mybir.dt.uint8
+FP8X4 = mybir.dt.float8_e4m3fn_x4
+FP4X4 = mybir.dt.float4_e2m1fn_x4
+ALU = mybir.AluOpType
+ACT = mybir.ActivationFunctionType
+
+P = 128
+T = 2048
+S = 512
+PACK = 4
+FLOPS = 3 * 2 * 512 * 512 * 512
+
+Z_CHUNKS = ((0, 256), (256, 512))
+OUT_CHUNKS = ((0, 256), (256, 384), (384, 512))
+
+
+def tile_picked_ccmpnormbwind_none_po_kernel(
+    tc, x_words, x_scales, w1_words, w1_scales, gs, offs, n1, n2, ca, cb, n3, n4, out_0, out_1, out_2
+):
+    nc = tc.nc
+    with ExitStack() as ctx:
+        keep = ctx.enter_context(tc.tile_pool(name="keep", bufs=1))
+        psum = ctx.enter_context(tc.psum_pool(name="psum", bufs=1))
+
+        def tile(name, shape, dtype, tag=None):
+            return keep.tile(shape, dtype, name=name, tag=tag or name, align_bytes=64)
+
+        def load_scale_rows(plane, rows):
+            for q in range(4):
+                nc.sync.dma_start(
+                    out=plane[32 * q : 32 * q + 4, :].bitcast(I32), in_=rows[0, 4 * q : 4 * q + 4, :].bitcast(I32)
+                )
+
+        def load_list(name, src):
+            lst = keep.tile([P, S // 16], U16, name=name)
+            nc.sync.dma_start(lst[:], src)
+            return lst
+
+        xs = tile("xs", [P, T], U8)
+        w1s_raw = tile("w1s_raw", [P, S], U8)
+        nc.vector.memset(xs[:].bitcast(I32), 0)
+        nc.vector.memset(w1s_raw[:].bitcast(I32), 0)
+        half = tile("half", [P, 1], F32)
+        nc.vector.memset(half[:], 0.5)
+        warm = tile("warm", [P, 1], F32)
+        nc.scalar.activation(warm[:], half[:], ACT.Abs_reciprocal_sqrt)
+
+        load_scale_rows(xs, x_scales)
+        offs_l = load_list("offs_l", offs)
+        cb_l = load_list("cb_l", cb)
+        w1w_raw = tile("w1w_raw", [P, 2 * S], U8)
+        nc.sync.dma_start(out=w1w_raw[:].bitcast(I32), in_=w1_words[0].bitcast(I32))
+        xw = tile("xw", [P, T], I32)
+        nc.sync.dma_start(out=xw[:], in_=x_words[0].rearrange("p n t -> p (n t)").bitcast(I32))
+        load_scale_rows(w1s_raw, w1_scales)
+        n2_l = load_list("n2_l", n2)
+        n1_l = load_list("n1_l", n1)
+        gs_sb = tile("gs_sb", [P, PACK], F32)
+        nc.sync.dma_start(out=gs_sb[:], in_=gs.rearrange("(p t) o -> p (t o)", t=PACK))
+        ca_l = load_list("ca_l", ca)
+        n4_l = load_list("n4_l", n4)
+        n3_l = load_list("n3_l", n3)
+
+        def gather_bytes(name, lst, tag=None):
+            got = tile(name, [P, S], U8, tag)
+            nc.vector.tensor_copy(got[:], xs[:].indirect(lst[:]))
+            return got
+
+        def deal_bytes(name, src, width):
+            dealt = tile(name, [P, S * width], U8)
+            nc.vector.tensor_copy(
+                dealt[:].rearrange("p (t m b) -> p m t b", t=PACK, b=width),
+                src[:].rearrange("p (m t b) -> p m t b", t=PACK, b=width),
+            )
+            return dealt
+
+        def gather_words(name, lst, dealt, tag=None):
+            got = tile(name, [P, S], U32, tag)
+            dst = got[:].rearrange("p (t m) -> p m t", t=PACK) if dealt else got[:]
+            nc.vector.tensor_copy(dst, xw[:].bitcast(U32).indirect(lst[:]))
+            return got
+
+        xq_s = gather_bytes("xq_s", offs_l)
+        w1w = deal_bytes("w1w", w1w_raw, 2)
+        cb_s_raw = gather_bytes("cb_s_raw", cb_l)
+        xq_w = gather_words("xq_w", offs_l, False)
+        w1s = deal_bytes("w1s", w1s_raw, 1)
+
+        banks_y = [psum.tile([P, S], F32, name=f"y_ps{t}", tag=f"lo{t}") for t in range(PACK)]
+        y = [tile(f"y{t}", [P, S], F32) for t in range(PACK)]
+        for t in range(PACK):
+            nc.tensor.matmul_mx(
+                out=banks_y[t][:],
+                lhsT=w1w[:, 256 * t : 256 * (t + 1)].bitcast(FP4X4),
+                lhsT_scale=w1s[:, P * t : P * (t + 1)],
+                rhs=xq_w[:].bitcast(FP8X4),
+                rhs_scale=xq_s[:],
+                start=True,
+                stop=True,
+            )
+            nc.scalar.copy(y[t][:], banks_y[t][:])
+
+        cb_w = gather_words("cb_w", cb_l, True, "w1s_raw")
+        cb_s = deal_bytes("cb_s", cb_s_raw, 1)
+
+        def offsets(lst, lo, hi):
+            return lst[:, lo // 16 : hi // 16]
+
+        banks_b = [psum.tile([P, S], F32, name=f"b_ps{t}", tag=f"hi{t}") for t in range(PACK)]
+        banks_a = [psum.tile([P, S], F32, name=f"a_ps{t}", tag=f"lo{t}") for t in range(PACK)]
+        babs = [tile(f"babs{t}", [P, S], F32) for t in range(PACK)]
+        a = [tile(f"a{t}", [P, S], F32) for t in range(PACK)]
+
+        def product(banks, words, scales, zq, lo, hi, t):
+            nc.tensor.matmul_mx(
+                out=banks[t][:, lo:hi],
+                lhsT=words[:, P * t : P * (t + 1)].bitcast(FP8X4),
+                lhsT_scale=scales[:, P * t : P * (t + 1)],
+                rhs=zq[0][:].bitcast(FP8X4),
+                rhs_scale=zq[1][:],
+                start=True,
+                stop=True,
+            )
+
+        zq = []
+        for c, (lo, hi) in enumerate(Z_CHUNKS):
+            w = hi - lo
+            y2 = tile(f"y2_{c}", [P, PACK, w], F32)
+            diff = tile(f"diff_{c}", [P, PACK, w], F32)
+            z = tile(f"z_{c}", [P, PACK, w], BF16)
+            for step in range(PACK + 2):
+                if step < PACK:
+                    t = step
+                    nc.vector.tensor_copy(y2[:, t, :], y[t][:].indirect(offsets(n2_l, lo, hi)))
+                if 1 <= step <= PACK:
+                    t = step - 1
+                    nc.vector.tensor_tensor(diff[:, t, :], y[t][:].indirect(offsets(n1_l, lo, hi)), y2[:, t, :], ALU.subtract)
+                if step >= 2:
+                    t = step - 2
+                    nc.vector.scalar_tensor_tensor(
+                        z[:, t, :], diff[:, t, :], gs_sb[:, t : t + 1], y[t][:, lo:hi], ALU.mult, ALU.mult
+                    )
+            zi = tile(f"zi_{c}", [P, w, PACK], BF16)
+            nc.scalar.copy(zi[:], z[:].rearrange("p t j -> p j t"))
+            if c == len(Z_CHUNKS) - 1:
+                ca_s_raw = gather_bytes("ca_s_raw", ca_l, f"y2_{c}")
+                ca_s = deal_bytes("ca_s", ca_s_raw, 1)
+            zw = tile(f"zw_{c}", [P, w], U32)
+            zs = tile(f"zs_{c}", [P, w], U8)
+            nc.vector.quantize_mx(out=zw[:].bitcast(FP8X4), scales=zs[:], in_=zi[:].rearrange("p j t -> p (j t)"))
+            zq.append((zw, zs))
+            for t in range(PACK):
+                product(banks_b, cb_w, cb_s, zq[c], lo, hi, t)
+                nc.scalar.activation(babs[t][:, lo:hi], banks_b[t][:, lo:hi], ACT.Abs, scale=0.0625)
+
+        ca_w = gather_words("ca_w", ca_l, True, f"zi_{len(Z_CHUNKS) - 1}")
+        for t in range(PACK):
+            for c, (lo, hi) in enumerate(Z_CHUNKS):
+                product(banks_a, ca_w, ca_s, zq[c], lo, hi, t)
+
+        recip = tile("recip", [P, PACK, S], F32)
+        b4 = tile("b4", [P, PACK, S], F32)
+        den = tile("den", [P, PACK, S], F32)
+        root = tile("root", [P, PACK, S], F32)
+        halves = ((0, 256), (256, 512))
+        for step in range(PACK + 1):
+            if step < PACK:
+                t = step
+                for lo, hi in halves:
+                    nc.vector.tensor_copy(b4[:, t, lo:hi], babs[t][:].indirect(offsets(n4_l, lo, hi)))
+                nc.scalar.activation(a[t][:], banks_a[t][:], ACT.Copy, scale=0.0625)
+            if step >= 1:
+                t = step - 1
+                nc.vector.tensor_tensor(den[:, t, :], b4[:, t, :], babs[t][:], ALU.add)
+                nc.scalar.activation(root[:, t, :], den[:, t, :], ACT.Abs_reciprocal_sqrt, bias=half[:])
+                nc.scalar.activation(recip[:, t, :], root[:, t, :], ACT.Square)
+
+        ow = tile("ow", [P, S], I32)
+        osc = tile("osc", [P, S], U8)
+        out_rows = out_0.rearrange("(p t) j -> p t j", t=PACK)
+        out_words = out_1[0].rearrange("p n t -> p (n t)").bitcast(I32)
+        pending = None
+
+        def finish(lo, hi, oi):
+            nc.vector.quantize_mx(
+                out=ow[:, lo:hi].bitcast(FP8X4), scales=osc[:, lo:hi], in_=oi[:].rearrange("p j t -> p (j t)")
+            )
+            nc.sync.dma_start(out=out_words[:, lo:hi], in_=ow[:, lo:hi])
+
+        for c, (lo, hi) in enumerate(OUT_CHUNKS):
+            w = hi - lo
+            a3 = tile(f"a3_{c}", [P, PACK, w], F32)
+            num = tile(f"num_{c}", [P, PACK, w], F32)
+            o = tile(f"o_{c}", [P, PACK, w], F32)
+            for step in range(PACK + 1):
+                if step < PACK:
+                    t = step
+                    nc.vector.tensor_copy(a3[:, t, :], a[t][:].indirect(offsets(n3_l, lo, hi)))
+                if step >= 1:
+                    t = step - 1
+                    nc.vector.tensor_tensor(num[:, t, :], a[t][:, lo:hi], a3[:, t, :], ALU.subtract)
+            if pending is not None:
+                finish(*pending)
+            nc.vector.tensor_tensor(o[:], num[:], recip[:, :, lo:hi], ALU.mult)
+            nc.sync.dma_start(out=out_rows[:, :, lo:hi], in_=o[:])
+            oi = tile(f"oi_{c}", [P, w, PACK], BF16)
+            nc.scalar.copy(oi[:], o[:].rearrange("p t j -> p j t"))
+            pending = (lo, hi, oi)
+        finish(*pending)
+        for q in range(4):
+            queue = nc.sync if q % 2 == 0 else nc.scalar
+            queue.dma_start(
+                out=out_2[0, 4 * q : 4 * q + 4, :].bitcast(I32), in_=osc[32 * q : 32 * q + 4, :].bitcast(I32)
+            )

@@ -17,6 +17,7 @@ P = 128
 T = 2048
 S = 512
 PACK = 4
+HALF = 256
 FLOPS = 3 * 2 * 512 * 512 * 512
 
 Z_CHUNKS = ((0, 256), (256, 512))
@@ -118,7 +119,9 @@ def tile_picked_ccmpnormbwind_none_po_kernel(
         banks_b = [psum.tile([P, S], F32, name=f"b_ps{t}", tag=f"hi{t}") for t in range(PACK)]
         banks_a = [psum.tile([P, S], F32, name=f"a_ps{t}", tag=f"lo{t}") for t in range(PACK)]
         babs = [tile(f"babs{t}", [P, S], F32) for t in range(PACK)]
+        babs_twin = [tile(f"babs_twin{t}", [P, S], F32) for t in range(PACK)]
         a = [tile(f"a{t}", [P, S], F32) for t in range(PACK)]
+        a_twin = [tile(f"a_twin{t}", [P, S], F32) for t in range(PACK)]
 
         def product(banks, words, scales, zq, lo, hi, t):
             nc.tensor.matmul_mx(
@@ -161,28 +164,30 @@ def tile_picked_ccmpnormbwind_none_po_kernel(
             for t in range(PACK):
                 product(banks_b, cb_w, cb_s, zq[c], lo, hi, t)
                 nc.scalar.activation(babs[t][:, lo:hi], banks_b[t][:, lo:hi], ACT.Abs, scale=0.0625)
+                nc.scalar.activation(babs_twin[t][:, lo:hi], banks_b[t][:, lo:hi], ACT.Abs, scale=0.0625)
 
         ca_w = gather_words("ca_w", ca_l, True, f"zi_{len(Z_CHUNKS) - 1}")
         for t in range(PACK):
             for c, (lo, hi) in enumerate(Z_CHUNKS):
                 product(banks_a, ca_w, ca_s, zq[c], lo, hi, t)
 
-        recip = tile("recip", [P, PACK, S], F32)
-        b4 = tile("b4", [P, PACK, S], F32)
-        den = tile("den", [P, PACK, S], F32)
-        root = tile("root", [P, PACK, S], F32)
-        halves = ((0, 256), (256, 512))
-        for step in range(PACK + 1):
-            if step < PACK:
-                t = step
-                for lo, hi in halves:
-                    nc.vector.tensor_copy(b4[:, t, lo:hi], babs[t][:].indirect(offsets(n4_l, lo, hi)))
-                nc.scalar.activation(a[t][:], banks_a[t][:], ACT.Copy, scale=0.0625)
-            if step >= 1:
-                t = step - 1
-                nc.vector.tensor_tensor(den[:, t, :], b4[:, t, :], babs[t][:], ALU.add)
-                nc.scalar.activation(root[:, t, :], den[:, t, :], ACT.Abs_reciprocal_sqrt, bias=half[:])
-                nc.scalar.activation(recip[:, t, :], root[:, t, :], ACT.Square)
+        for t in range(PACK):
+            nc.scalar.activation(a[t][:], banks_a[t][:], ACT.Copy, scale=-0.0625)
+            nc.sync.dma_start(out=a_twin[t][:], in_=a[t][:])
+
+        recip = []
+        for h in range(2):
+            lo, hi = HALF * h, HALF * (h + 1)
+            den = tile(f"den{h}", [P, PACK, HALF], F32)
+            for t in range(PACK):
+                nc.vector.tensor_tensor(
+                    den[:, t, :], babs[t][:].indirect(offsets(n4_l, lo, hi)), babs_twin[t][:, lo:hi], ALU.add
+                )
+            root = tile(f"root{h}", [P, PACK, HALF], F32)
+            nc.scalar.activation(root[:], den[:], ACT.Abs_reciprocal_sqrt, bias=half[:])
+            rec = tile(f"recip{h}", [P, PACK, HALF], F32)
+            nc.scalar.activation(rec[:], root[:], ACT.Square)
+            recip.append(rec)
 
         ow = tile("ow", [P, S], I32)
         osc = tile("osc", [P, S], U8)
@@ -198,19 +203,15 @@ def tile_picked_ccmpnormbwind_none_po_kernel(
 
         for c, (lo, hi) in enumerate(OUT_CHUNKS):
             w = hi - lo
-            a3 = tile(f"a3_{c}", [P, PACK, w], F32)
             num = tile(f"num_{c}", [P, PACK, w], F32)
             o = tile(f"o_{c}", [P, PACK, w], F32)
-            for step in range(PACK + 1):
-                if step < PACK:
-                    t = step
-                    nc.vector.tensor_copy(a3[:, t, :], a[t][:].indirect(offsets(n3_l, lo, hi)))
-                if step >= 1:
-                    t = step - 1
-                    nc.vector.tensor_tensor(num[:, t, :], a[t][:, lo:hi], a3[:, t, :], ALU.subtract)
+            for t in range(PACK):
+                nc.vector.tensor_tensor(
+                    num[:, t, :], a[t][:].indirect(offsets(n3_l, lo, hi)), a_twin[t][:, lo:hi], ALU.subtract
+                )
             if pending is not None:
                 finish(*pending)
-            nc.vector.tensor_tensor(o[:], num[:], recip[:, :, lo:hi], ALU.mult)
+            nc.vector.tensor_tensor(o[:], num[:], recip[lo // HALF][:, :, lo % HALF : lo % HALF + w], ALU.mult)
             nc.sync.dma_start(out=out_rows[:, :, lo:hi], in_=o[:])
             oi = tile(f"oi_{c}", [P, w, PACK], BF16)
             nc.scalar.copy(oi[:], o[:].rearrange("p t j -> p j t"))

@@ -16,12 +16,11 @@ ACT = mybir.ActivationFunctionType
 P = 128
 T = 2048
 S = 512
-PACK = 4
-HALF = 256
+SLOTS = 4
+HALF = S // 2
+QUARTER = S // 4
+X_FIRST = 768
 FLOPS = 3 * 2 * 512 * 512 * 512
-
-Z_CHUNKS = ((0, 256), (256, 512))
-OUT_CHUNKS = ((0, 256), (256, 384), (384, 512))
 
 
 def tile_picked_ccmpnormbwind_none_po_kernel(
@@ -32,193 +31,220 @@ def tile_picked_ccmpnormbwind_none_po_kernel(
         keep = ctx.enter_context(tc.tile_pool(name="keep", bufs=1))
         psum = ctx.enter_context(tc.psum_pool(name="psum", bufs=1))
 
-        def tile(name, shape, dtype, tag=None):
-            return keep.tile(shape, dtype, name=name, tag=tag or name, align_bytes=64)
+        def tile(name, shape, dtype, after=None):
+            return keep.tile(shape, dtype, name=name, tag=after or name, align_bytes=64)
 
-        def load_scale_rows(plane, rows):
-            for q in range(4):
-                nc.sync.dma_start(
-                    out=plane[32 * q : 32 * q + 4, :].bitcast(I32), in_=rows[0, 4 * q : 4 * q + 4, :].bitcast(I32)
-                )
+        def slots(name):
+            return [tile(f"{name}{t}", [P, S], F32) for t in range(SLOTS)]
+
+        def columns(h):
+            return slice(HALF * h, HALF * (h + 1))
+
+        def looked_up(window, lst, h):
+            return window[:].indirect(lst[:, HALF * h // 16 : HALF * (h + 1) // 16])
 
         def load_list(name, src):
             lst = keep.tile([P, S // 16], U16, name=name)
             nc.sync.dma_start(lst[:], src)
             return lst
 
-        xs = tile("xs", [P, T], U8)
-        w1s_raw = tile("w1s_raw", [P, S], U8)
-        nc.vector.memset(xs[:].bitcast(I32), 0)
-        nc.vector.memset(w1s_raw[:].bitcast(I32), 0)
-        half = tile("half", [P, 1], F32)
-        nc.vector.memset(half[:], 0.5)
-        warm = tile("warm", [P, 1], F32)
-        nc.scalar.activation(warm[:], half[:], ACT.Abs_reciprocal_sqrt)
+        def load_scale_rows(plane, rows, queues):
+            for q in range(4):
+                queues[q % len(queues)].dma_start(
+                    out=plane[32 * q : 32 * q + 4, :].bitcast(I32), in_=rows[0, 4 * q : 4 * q + 4, :].bitcast(I32)
+                )
 
-        load_scale_rows(xs, x_scales)
+        x_s = tile("x_s", [P, T], U8)
+        w1_s_raw = tile("w1_s_raw", [P, S], U8)
+        nc.vector.memset(x_s[:].bitcast(I32), 0)
+        nc.vector.memset(w1_s_raw[:].bitcast(I32), 0)
+
+        w1_w_raw = tile("w1_w_raw", [P, 2 * S], U8)
+        nc.sync.dma_start(out=w1_w_raw[:].bitcast(I32), in_=w1_words[0].bitcast(I32))
         offs_l = load_list("offs_l", offs)
+        x_w = tile("x_w", [P, T], I32)
+        x_rows = x_words[0].rearrange("p n t -> p (n t)").bitcast(I32)
+        nc.sync.dma_start(out=x_w[:, 0:X_FIRST], in_=x_rows[:, 0:X_FIRST])
+        load_scale_rows(x_s, x_scales, (nc.sync, nc.scalar))
+        nc.sync.dma_start(out=x_w[:, X_FIRST:T], in_=x_rows[:, X_FIRST:T])
+        gs_sb = tile("gs_sb", [P, SLOTS], F32)
+        nc.sync.dma_start(out=gs_sb[:], in_=gs.rearrange("(p t) o -> p (t o)", t=SLOTS))
+        load_scale_rows(w1_s_raw, w1_scales, (nc.sync,))
         cb_l = load_list("cb_l", cb)
-        w1w_raw = tile("w1w_raw", [P, 2 * S], U8)
-        nc.sync.dma_start(out=w1w_raw[:].bitcast(I32), in_=w1_words[0].bitcast(I32))
-        xw = tile("xw", [P, T], I32)
-        nc.sync.dma_start(out=xw[:], in_=x_words[0].rearrange("p n t -> p (n t)").bitcast(I32))
-        load_scale_rows(w1s_raw, w1_scales)
-        n2_l = load_list("n2_l", n2)
         n1_l = load_list("n1_l", n1)
-        gs_sb = tile("gs_sb", [P, PACK], F32)
-        nc.sync.dma_start(out=gs_sb[:], in_=gs.rearrange("(p t) o -> p (t o)", t=PACK))
+        n2_l = load_list("n2_l", n2)
         ca_l = load_list("ca_l", ca)
         n4_l = load_list("n4_l", n4)
         n3_l = load_list("n3_l", n3)
 
-        def gather_bytes(name, lst, tag=None):
-            got = tile(name, [P, S], U8, tag)
-            nc.vector.tensor_copy(got[:], xs[:].indirect(lst[:]))
+        def gather_bytes(name, lst, after=None):
+            got = tile(name, [P, S], U8, after)
+            nc.vector.tensor_copy(got[:], x_s[:].indirect(lst[:]))
+            return got
+
+        def gather_words(dst, lst):
+            nc.vector.tensor_copy(dst, x_w[:].bitcast(U32).indirect(lst[:]))
+
+        def gather_dealt_words(name, lst, after=None):
+            got = tile(name, [P, S], U32, after)
+            gather_words(got[:].rearrange("p (t m) -> p m t", t=SLOTS), lst)
             return got
 
         def deal_bytes(name, src, width):
             dealt = tile(name, [P, S * width], U8)
             nc.vector.tensor_copy(
-                dealt[:].rearrange("p (t m b) -> p m t b", t=PACK, b=width),
-                src[:].rearrange("p (m t b) -> p m t b", t=PACK, b=width),
+                dealt[:].rearrange("p (t m b) -> p t m b", t=SLOTS, b=width),
+                src[:].rearrange("p (m t b) -> p t m b", t=SLOTS, b=width),
             )
             return dealt
 
-        def gather_words(name, lst, dealt, tag=None):
-            got = tile(name, [P, S], U32, tag)
-            dst = got[:].rearrange("p (t m) -> p m t", t=PACK) if dealt else got[:]
-            nc.vector.tensor_copy(dst, xw[:].bitcast(U32).indirect(lst[:]))
-            return got
-
+        w1_w = deal_bytes("w1_w", w1_w_raw, 2)
+        four = tile("four", [P, 1], F32, "w1_w_raw")
+        nc.vector.memset(four[:], 4.0)
+        one_half = tile("one_half", [P, 1], F32)
+        nc.scalar.activation(one_half[:], four[:], ACT.Abs_reciprocal_sqrt)
         xq_s = gather_bytes("xq_s", offs_l)
-        w1w = deal_bytes("w1w", w1w_raw, 2)
-        cb_s_raw = gather_bytes("cb_s_raw", cb_l)
-        xq_w = gather_words("xq_w", offs_l, False)
-        w1s = deal_bytes("w1s", w1s_raw, 1)
+        xq_w = tile("xq_w", [P, S], U32)
+        gather_words(xq_w[:], offs_l)
+        w1_s = deal_bytes("w1_s", w1_s_raw, 1)
 
-        banks_y = [psum.tile([P, S], F32, name=f"y_ps{t}", tag=f"lo{t}") for t in range(PACK)]
-        y = [tile(f"y{t}", [P, S], F32) for t in range(PACK)]
-        for t in range(PACK):
+        y_ps = [psum.tile([P, S], F32, name=f"y_ps{t}", tag=f"y_then_a{t}") for t in range(SLOTS)]
+        y = slots("y")
+        gy = [tile(f"gy{h}", [P, SLOTS, HALF], F32) for h in range(2)]
+
+        def weigh(h, t):
+            nc.scalar.activation(gy[h][:, t, :], y_ps[t][:, columns(h)], ACT.Copy, scale=gs_sb[:, t : t + 1])
+
+        for t in range(SLOTS):
             nc.tensor.matmul_mx(
-                out=banks_y[t][:],
-                lhsT=w1w[:, 256 * t : 256 * (t + 1)].bitcast(FP4X4),
-                lhsT_scale=w1s[:, P * t : P * (t + 1)],
+                out=y_ps[t][:],
+                lhsT=w1_w[:, 2 * P * t : 2 * P * (t + 1)].bitcast(FP4X4),
+                lhsT_scale=w1_s[:, P * t : P * (t + 1)],
                 rhs=xq_w[:].bitcast(FP8X4),
                 rhs_scale=xq_s[:],
                 start=True,
                 stop=True,
             )
-            nc.scalar.copy(y[t][:], banks_y[t][:])
+            nc.scalar.copy(y[t][:], y_ps[t][:])
+            weigh(0, t)
+        for t in range(SLOTS):
+            weigh(1, t)
 
-        cb_w = gather_words("cb_w", cb_l, True, "w1s_raw")
-        cb_s = deal_bytes("cb_s", cb_s_raw, 1)
+        cb_w = gather_dealt_words("cb_w", cb_l)
+        cb_s = deal_bytes("cb_s", gather_bytes("cb_s_raw", cb_l, "w1_s_raw"), 1)
 
-        def offsets(lst, lo, hi):
-            return lst[:, lo // 16 : hi // 16]
+        b_ps = [psum.tile([P, S], F32, name=f"b_ps{t}") for t in range(SLOTS)]
+        b_abs, b_twin = slots("b_abs"), slots("b_twin")
+        z_q = []
 
-        banks_b = [psum.tile([P, S], F32, name=f"b_ps{t}", tag=f"hi{t}") for t in range(PACK)]
-        banks_a = [psum.tile([P, S], F32, name=f"a_ps{t}", tag=f"lo{t}") for t in range(PACK)]
-        babs = [tile(f"babs{t}", [P, S], F32) for t in range(PACK)]
-        babs_twin = [tile(f"babs_twin{t}", [P, S], F32) for t in range(PACK)]
-        a = [tile(f"a{t}", [P, S], F32) for t in range(PACK)]
-        a_twin = [tile(f"a_twin{t}", [P, S], F32) for t in range(PACK)]
+        def times_gy(dst, lst, h, t):
+            nc.vector.tensor_tensor(dst[:, t, :], looked_up(y[t], lst, h), gy[h][:, t, :], ALU.mult)
 
-        def product(banks, words, scales, zq, lo, hi, t):
+        def interleave(name, src):
+            side_by_side = tile(name, [P, HALF, SLOTS], BF16)
+            nc.scalar.copy(side_by_side[:], src[:].rearrange("p t j -> p j t"))
+            return side_by_side
+
+        def quantise(words, scales, side_by_side):
+            nc.vector.quantize_mx(
+                out=words.bitcast(FP8X4), scales=scales, in_=side_by_side[:].rearrange("p j t -> p (j t)")
+            )
+
+        def score(banks, words, scales, h, t):
             nc.tensor.matmul_mx(
-                out=banks[t][:, lo:hi],
+                out=banks[t][:, columns(h)],
                 lhsT=words[:, P * t : P * (t + 1)].bitcast(FP8X4),
                 lhsT_scale=scales[:, P * t : P * (t + 1)],
-                rhs=zq[0][:].bitcast(FP8X4),
-                rhs_scale=zq[1][:],
+                rhs=z_q[h][0][:].bitcast(FP8X4),
+                rhs_scale=z_q[h][1][:],
                 start=True,
                 stop=True,
             )
 
-        zq = []
-        for c, (lo, hi) in enumerate(Z_CHUNKS):
-            w = hi - lo
-            y2 = tile(f"y2_{c}", [P, PACK, w], F32)
-            diff = tile(f"diff_{c}", [P, PACK, w], F32)
-            z = tile(f"z_{c}", [P, PACK, w], BF16)
-            for step in range(PACK + 2):
-                if step < PACK:
-                    t = step
-                    nc.vector.tensor_copy(y2[:, t, :], y[t][:].indirect(offsets(n2_l, lo, hi)))
-                if 1 <= step <= PACK:
-                    t = step - 1
-                    nc.vector.tensor_tensor(diff[:, t, :], y[t][:].indirect(offsets(n1_l, lo, hi)), y2[:, t, :], ALU.subtract)
-                if step >= 2:
-                    t = step - 2
-                    nc.vector.scalar_tensor_tensor(
-                        z[:, t, :], diff[:, t, :], gs_sb[:, t : t + 1], y[t][:, lo:hi], ALU.mult, ALU.mult
-                    )
-            zi = tile(f"zi_{c}", [P, w, PACK], BF16)
-            nc.scalar.copy(zi[:], z[:].rearrange("p t j -> p j t"))
-            if c == len(Z_CHUNKS) - 1:
-                ca_s_raw = gather_bytes("ca_s_raw", ca_l, f"y2_{c}")
-                ca_s = deal_bytes("ca_s", ca_s_raw, 1)
-            zw = tile(f"zw_{c}", [P, w], U32)
-            zs = tile(f"zs_{c}", [P, w], U8)
-            nc.vector.quantize_mx(out=zw[:].bitcast(FP8X4), scales=zs[:], in_=zi[:].rearrange("p j t -> p (j t)"))
-            zq.append((zw, zs))
-            for t in range(PACK):
-                product(banks_b, cb_w, cb_s, zq[c], lo, hi, t)
-                nc.scalar.activation(babs[t][:, lo:hi], banks_b[t][:, lo:hi], ACT.Abs, scale=0.0625)
-                nc.scalar.activation(babs_twin[t][:, lo:hi], banks_b[t][:, lo:hi], ACT.Abs, scale=0.0625)
+        def size_of_b(dst, h, t):
+            nc.scalar.activation(dst[t][:, columns(h)], b_ps[t][:, columns(h)], ACT.Abs, scale=0.0625)
 
-        ca_w = gather_words("ca_w", ca_l, True, f"zi_{len(Z_CHUNKS) - 1}")
-        for t in range(PACK):
-            for c, (lo, hi) in enumerate(Z_CHUNKS):
-                product(banks_a, ca_w, ca_s, zq[c], lo, hi, t)
+        def quantise_z_and_score_b(h, side_by_side):
+            z_q.append((tile(f"z_w{h}", [P, HALF], U32), tile(f"z_s{h}", [P, HALF], U8)))
+            quantise(z_q[h][0][:], z_q[h][1][:], side_by_side)
+            for t in range(SLOTS):
+                score(b_ps, cb_w, cb_s, h, t)
+                size_of_b(b_abs, h, t)
 
-        for t in range(PACK):
-            nc.scalar.activation(a[t][:], banks_a[t][:], ACT.Copy, scale=-0.0625)
-            nc.sync.dma_start(out=a_twin[t][:], in_=a[t][:])
+        z = [tile(f"z{h}", [P, SLOTS, HALF], BF16) for h in range(2)]
+        by_n1 = [tile(f"by_n1_{h}", [P, SLOTS, HALF], F32) for h in range(2)]
+        by_n2_first = tile("by_n2_first", [P, SLOTS, HALF], F32)
+        for t in range(SLOTS):
+            times_gy(by_n1[0], n1_l, 0, t)
+            times_gy(by_n2_first, n2_l, 0, t)
+        times_gy(by_n1[1], n1_l, 1, 0)
+        nc.vector.tensor_tensor(z[0][:], by_n1[0][:], by_n2_first[:], ALU.subtract)
+        z_side = interleave("z_side0", z[0])
+        for t in range(1, SLOTS):
+            times_gy(by_n1[1], n1_l, 1, t)
+        quantise_z_and_score_b(0, z_side)
+        for t in range(SLOTS):
+            nc.sync.dma_start(out=b_twin[t][:, columns(0)], in_=b_abs[t][:, columns(0)])
+        by_n2_second = tile("by_n2_second", [P, SLOTS, HALF], F32, "z0")
+        for t in range(SLOTS):
+            times_gy(by_n2_second, n2_l, 1, t)
+        for some in (slice(0, SLOTS - 1), slice(SLOTS - 1, SLOTS)):
+            nc.vector.tensor_tensor(z[1][:, some, :], by_n1[1][:, some, :], by_n2_second[:, some, :], ALU.subtract)
+        z_side = interleave("z_side1", z[1])
 
-        recip = []
+        ca_s = deal_bytes("ca_s", gather_bytes("ca_s_raw", ca_l, "gy1"), 1)
+        quantise_z_and_score_b(1, z_side)
+        ca_w = gather_dealt_words("ca_w", ca_l, "z1")
+
+        a_ps = [psum.tile([P, S], F32, name=f"a_ps{t}", tag=f"y_then_a{t}") for t in range(SLOTS)]
+        a_neg, a_twin = slots("a_neg"), slots("a_twin")
+        for t in range(SLOTS):
+            for h in range(2):
+                score(a_ps, ca_w, ca_s, h, t)
+            size_of_b(b_twin, 1, t)
+            nc.scalar.activation(a_neg[t][:], a_ps[t][:], ACT.Copy, scale=-0.0625)
+            nc.sync.dma_start(out=a_twin[t][:], in_=a_neg[t][:])
+
+        inverse = []
         for h in range(2):
-            lo, hi = HALF * h, HALF * (h + 1)
-            den = tile(f"den{h}", [P, PACK, HALF], F32)
-            for t in range(PACK):
+            sizes = tile(f"sizes{h}", [P, SLOTS, HALF], F32)
+            for t in range(SLOTS):
+                nc.vector.tensor_tensor(sizes[:, t, :], looked_up(b_abs[t], n4_l, h), b_twin[t][:, columns(h)], ALU.add)
+            root = tile(f"root{h}", [P, SLOTS, HALF], F32)
+            nc.scalar.activation(root[:], sizes[:], ACT.Abs_reciprocal_sqrt, bias=one_half[:])
+            inverse.append(tile(f"inverse{h}", [P, SLOTS, HALF], F32))
+            nc.scalar.activation(inverse[h][:], root[:], ACT.Square)
+
+        numerator = [tile(f"numerator{h}", [P, SLOTS, HALF], F32) for h in range(2)]
+        for t in range(SLOTS):
+            for h in range(2):
                 nc.vector.tensor_tensor(
-                    den[:, t, :], babs[t][:].indirect(offsets(n4_l, lo, hi)), babs_twin[t][:, lo:hi], ALU.add
+                    numerator[h][:, t, :], looked_up(a_neg[t], n3_l, h), a_twin[t][:, columns(h)], ALU.subtract
                 )
-            root = tile(f"root{h}", [P, PACK, HALF], F32)
-            nc.scalar.activation(root[:], den[:], ACT.Abs_reciprocal_sqrt, bias=half[:])
-            rec = tile(f"recip{h}", [P, PACK, HALF], F32)
-            nc.scalar.activation(rec[:], root[:], ACT.Square)
-            recip.append(rec)
 
-        ow = tile("ow", [P, S], I32)
-        osc = tile("osc", [P, S], U8)
-        out_rows = out_0.rearrange("(p t) j -> p t j", t=PACK)
-        out_words = out_1[0].rearrange("p n t -> p (n t)").bitcast(I32)
-        pending = None
+        out_rows = out_0.rearrange("(p t) j -> p t j", t=SLOTS)
 
-        def finish(lo, hi, oi):
-            nc.vector.quantize_mx(
-                out=ow[:, lo:hi].bitcast(FP8X4), scales=osc[:, lo:hi], in_=oi[:].rearrange("p j t -> p (j t)")
+        def divide(name, h, lo, hi):
+            got = tile(name, [P, SLOTS, hi - lo], F32)
+            nc.vector.tensor_tensor(got[:], numerator[h][:, :, lo:hi], inverse[h][:, :, lo:hi], ALU.mult)
+            nc.sync.dma_start(out=out_rows[:, :, HALF * h + lo : HALF * h + hi], in_=got[:])
+            return got
+
+        out_side = [interleave("out_side0", divide("out_first", 0, 0, HALF)), tile("out_side1", [P, HALF, SLOTS], BF16)]
+        quarters = [divide(f"out_quarter{i}", 1, QUARTER * i, QUARTER * (i + 1)) for i in range(2)]
+        for i in range(2):
+            nc.vector.tensor_copy(
+                out_side[1][:, QUARTER * i : QUARTER * (i + 1), :], quarters[i][:].rearrange("p t j -> p j t")
             )
-            nc.sync.dma_start(out=out_words[:, lo:hi], in_=ow[:, lo:hi])
 
-        for c, (lo, hi) in enumerate(OUT_CHUNKS):
-            w = hi - lo
-            num = tile(f"num_{c}", [P, PACK, w], F32)
-            o = tile(f"o_{c}", [P, PACK, w], F32)
-            for t in range(PACK):
-                nc.vector.tensor_tensor(
-                    num[:, t, :], a[t][:].indirect(offsets(n3_l, lo, hi)), a_twin[t][:, lo:hi], ALU.subtract
-                )
-            if pending is not None:
-                finish(*pending)
-            nc.vector.tensor_tensor(o[:], num[:], recip[lo // HALF][:, :, lo % HALF : lo % HALF + w], ALU.mult)
-            nc.sync.dma_start(out=out_rows[:, :, lo:hi], in_=o[:])
-            oi = tile(f"oi_{c}", [P, w, PACK], BF16)
-            nc.scalar.copy(oi[:], o[:].rearrange("p t j -> p j t"))
-            pending = (lo, hi, oi)
-        finish(*pending)
+        out_w = tile("out_w", [P, S], I32)
+        out_s = tile("out_s", [P, S], U8)
+        word_rows = out_1[0].rearrange("p n t -> p (n t)").bitcast(I32)
+        for h in range(2):
+            quantise(out_w[:, columns(h)], out_s[:, columns(h)], out_side[h])
+            nc.sync.dma_start(out=word_rows[:, columns(h)], in_=out_w[:, columns(h)])
         for q in range(4):
-            queue = nc.sync if q % 2 == 0 else nc.scalar
+            queue = nc.scalar if q % 2 == 0 else nc.sync
             queue.dma_start(
-                out=out_2[0, 4 * q : 4 * q + 4, :].bitcast(I32), in_=osc[32 * q : 32 * q + 4, :].bitcast(I32)
+                out=out_2[0, 4 * q : 4 * q + 4, :].bitcast(I32), in_=out_s[32 * q : 32 * q + 4, :].bitcast(I32)
             )

@@ -48,9 +48,9 @@ def tile_picked_ccmpnormbwind_none_po_kernel(
             nc.sync.dma_start(lst[:], src)
             return lst
 
-        def load_scale_rows(plane, rows, queues):
+        def load_scale_rows(plane, rows):
             for q in range(4):
-                queues[q % len(queues)].dma_start(
+                nc.sync.dma_start(
                     out=plane[32 * q : 32 * q + 4, :].bitcast(I32), in_=rows[0, 4 * q : 4 * q + 4, :].bitcast(I32)
                 )
 
@@ -58,6 +58,10 @@ def tile_picked_ccmpnormbwind_none_po_kernel(
         w1_s_raw = tile("w1_s_raw", [P, S], U8)
         nc.vector.memset(x_s[:].bitcast(I32), 0)
         nc.vector.memset(w1_s_raw[:].bitcast(I32), 0)
+        four = tile("four", [P, 1], F32)
+        nc.vector.memset(four[:], 4.0)
+        one_half = tile("one_half", [P, 1], F32)
+        nc.scalar.activation(one_half[:], four[:], ACT.Abs_reciprocal_sqrt)
 
         w1_w_raw = tile("w1_w_raw", [P, 2 * S], U8)
         nc.sync.dma_start(out=w1_w_raw[:].bitcast(I32), in_=w1_words[0].bitcast(I32))
@@ -65,11 +69,11 @@ def tile_picked_ccmpnormbwind_none_po_kernel(
         x_w = tile("x_w", [P, T], I32)
         x_rows = x_words[0].rearrange("p n t -> p (n t)").bitcast(I32)
         nc.sync.dma_start(out=x_w[:, 0:X_FIRST], in_=x_rows[:, 0:X_FIRST])
-        load_scale_rows(x_s, x_scales, (nc.sync, nc.scalar))
+        load_scale_rows(x_s, x_scales)
         nc.sync.dma_start(out=x_w[:, X_FIRST:T], in_=x_rows[:, X_FIRST:T])
         gs_sb = tile("gs_sb", [P, SLOTS], F32)
         nc.sync.dma_start(out=gs_sb[:], in_=gs.rearrange("(p t) o -> p (t o)", t=SLOTS))
-        load_scale_rows(w1_s_raw, w1_scales, (nc.sync,))
+        load_scale_rows(w1_s_raw, w1_scales)
         cb_l = load_list("cb_l", cb)
         n1_l = load_list("n1_l", n1)
         n2_l = load_list("n2_l", n2)
@@ -99,10 +103,6 @@ def tile_picked_ccmpnormbwind_none_po_kernel(
             return dealt
 
         w1_w = deal_bytes("w1_w", w1_w_raw, 2)
-        four = tile("four", [P, 1], F32, "w1_w_raw")
-        nc.vector.memset(four[:], 4.0)
-        one_half = tile("one_half", [P, 1], F32)
-        nc.scalar.activation(one_half[:], four[:], ACT.Abs_reciprocal_sqrt)
         xq_s = gather_bytes("xq_s", offs_l)
         xq_w = tile("xq_w", [P, S], U32)
         gather_words(xq_w[:], offs_l)

from contextlib import ExitStack

import concourse.mybir as mybir

F32 = mybir.dt.float32
BF16 = mybir.dt.bfloat16
I32 = mybir.dt.int32
U32 = mybir.dt.uint32
U16 = mybir.dt.uint16
U8 = mybir.dt.uint8
FP8X4 = mybir.dt.float8_e4m3fn_x4
FP4X4 = mybir.dt.float4_e2m1fn_x4
ALU = mybir.AluOpType
ACT = mybir.ActivationFunctionType

P = 128
T = 2048
S = 512
SLOTS = 4
HALF = S // 2
QUARTER = S // 4
X_FIRST = 768
FLOPS = 3 * 2 * 512 * 512 * 512


def tile_picked_ccmpnormbwind_none_po_kernel(
    tc, x_words, x_scales, w1_words, w1_scales, gs, offs, n1, n2, ca, cb, n3, n4, out_0, out_1, out_2
):
    nc = tc.nc
    with ExitStack() as ctx:
        keep = ctx.enter_context(tc.tile_pool(name="keep", bufs=1))
        psum = ctx.enter_context(tc.psum_pool(name="psum", bufs=1))

        def tile(name, shape, dtype, after=None):
            return keep.tile(shape, dtype, name=name, tag=after or name, align_bytes=64)

        def slots(name):
            return [tile(f"{name}{t}", [P, S], F32) for t in range(SLOTS)]

        def columns(h):
            return slice(HALF * h, HALF * (h + 1))

        def looked_up(window, lst, h):
            return window[:].indirect(lst[:, HALF * h // 16 : HALF * (h + 1) // 16])

        def load_list(name, src):
            lst = keep.tile([P, S // 16], U16, name=name)
            nc.sync.dma_start(lst[:], src)
            return lst

        def load_scale_rows(plane, rows):
            for q in range(4):
                nc.sync.dma_start(
                    out=plane[32 * q : 32 * q + 4, :].bitcast(I32), in_=rows[0, 4 * q : 4 * q + 4, :].bitcast(I32)
                )

        x_s = tile("x_s", [P, T], U8)
        w1_s_raw = tile("w1_s_raw", [P, S], U8)
        nc.vector.memset(x_s[:].bitcast(I32), 0)
        nc.vector.memset(w1_s_raw[:].bitcast(I32), 0)
        four = tile("four", [P, 1], F32)
        nc.vector.memset(four[:], 4.0)
        one_half = tile("one_half", [P, 1], F32)
        nc.scalar.activation(one_half[:], four[:], ACT.Abs_reciprocal_sqrt)

        w1_w_raw = tile("w1_w_raw", [P, 2 * S], U8)
        nc.sync.dma_start(out=w1_w_raw[:].bitcast(I32), in_=w1_words[0].bitcast(I32))
        offs_l = load_list("offs_l", offs)
        x_w = tile("x_w", [P, T], I32)
        x_rows = x_words[0].rearrange("p n t -> p (n t)").bitcast(I32)
        nc.sync.dma_start(out=x_w[:, 0:X_FIRST], in_=x_rows[:, 0:X_FIRST])
        load_scale_rows(x_s, x_scales)
        nc.sync.dma_start(out=x_w[:, X_FIRST:T], in_=x_rows[:, X_FIRST:T])
        gs_sb = tile("gs_sb", [P, SLOTS], F32)
        nc.sync.dma_start(out=gs_sb[:], in_=gs.rearrange("(p t) o -> p (t o)", t=SLOTS))
        load_scale_rows(w1_s_raw, w1_scales)
        cb_l = load_list("cb_l", cb)
        n1_l = load_list("n1_l", n1)
        n2_l = load_list("n2_l", n2)
        ca_l = load_list("ca_l", ca)
        n4_l = load_list("n4_l", n4)
        n3_l = load_list("n3_l", n3)

        def gather_bytes(name, lst, after=None):
            got = tile(name, [P, S], U8, after)
            nc.vector.tensor_copy(got[:], x_s[:].indirect(lst[:]))
            return got

        def gather_words(dst, lst):
            nc.vector.tensor_copy(dst, x_w[:].bitcast(U32).indirect(lst[:]))

        def gather_dealt_words(name, lst, after=None):
            got = tile(name, [P, S], U32, after)
            gather_words(got[:].rearrange("p (t m) -> p m t", t=SLOTS), lst)
            return got

        def deal_bytes(name, src, width):
            dealt = tile(name, [P, S * width], U8)
            nc.vector.tensor_copy(
                dealt[:].rearrange("p (t m b) -> p t m b", t=SLOTS, b=width),
                src[:].rearrange("p (m t b) -> p t m b", t=SLOTS, b=width),
            )
            return dealt

        w1_w = deal_bytes("w1_w", w1_w_raw, 2)
        xq_s = gather_bytes("xq_s", offs_l)
        xq_w = tile("xq_w", [P, S], U32)
        gather_words(xq_w[:], offs_l)
        w1_s = deal_bytes("w1_s", w1_s_raw, 1)

        y_ps = [psum.tile([P, S], F32, name=f"y_ps{t}", tag=f"y_then_a{t}") for t in range(SLOTS)]
        y = slots("y")
        gy = [tile(f"gy{h}", [P, SLOTS, HALF], F32) for h in range(2)]

        def weigh(h, t):
            nc.scalar.activation(gy[h][:, t, :], y_ps[t][:, columns(h)], ACT.Copy, scale=gs_sb[:, t : t + 1])

        for t in range(SLOTS):
            nc.tensor.matmul_mx(
                out=y_ps[t][:],
                lhsT=w1_w[:, 2 * P * t : 2 * P * (t + 1)].bitcast(FP4X4),
                lhsT_scale=w1_s[:, P * t : P * (t + 1)],
                rhs=xq_w[:].bitcast(FP8X4),
                rhs_scale=xq_s[:],
                start=True,
                stop=True,
            )
            nc.scalar.copy(y[t][:], y_ps[t][:])
            weigh(0, t)
        for t in range(SLOTS):
            weigh(1, t)

        cb_w = gather_dealt_words("cb_w", cb_l)
        cb_s = deal_bytes("cb_s", gather_bytes("cb_s_raw", cb_l, "w1_s_raw"), 1)

        b_ps = [psum.tile([P, S], F32, name=f"b_ps{t}") for t in range(SLOTS)]
        b_abs, b_twin = slots("b_abs"), slots("b_twin")
        z_q = []

        def times_gy(dst, lst, h, t):
            nc.vector.tensor_tensor(dst[:, t, :], looked_up(y[t], lst, h), gy[h][:, t, :], ALU.mult)

        def interleave(name, src):
            side_by_side = tile(name, [P, HALF, SLOTS], BF16)
            nc.scalar.copy(side_by_side[:], src[:].rearrange("p t j -> p j t"))
            return side_by_side

        def quantise(words, scales, side_by_side):
            nc.vector.quantize_mx(
                out=words.bitcast(FP8X4), scales=scales, in_=side_by_side[:].rearrange("p j t -> p (j t)")
            )

        def score(banks, words, scales, h, t):
            nc.tensor.matmul_mx(
                out=banks[t][:, columns(h)],
                lhsT=words[:, P * t : P * (t + 1)].bitcast(FP8X4),
                lhsT_scale=scales[:, P * t : P * (t + 1)],
                rhs=z_q[h][0][:].bitcast(FP8X4),
                rhs_scale=z_q[h][1][:],
                start=True,
                stop=True,
            )

        def size_of_b(dst, h, t):
            nc.scalar.activation(dst[t][:, columns(h)], b_ps[t][:, columns(h)], ACT.Abs, scale=0.0625)

        def quantise_z_and_score_b(h, side_by_side):
            z_q.append((tile(f"z_w{h}", [P, HALF], U32), tile(f"z_s{h}", [P, HALF], U8)))
            quantise(z_q[h][0][:], z_q[h][1][:], side_by_side)
            for t in range(SLOTS):
                score(b_ps, cb_w, cb_s, h, t)
                size_of_b(b_abs, h, t)

        z = [tile(f"z{h}", [P, SLOTS, HALF], BF16) for h in range(2)]
        by_n1 = [tile(f"by_n1_{h}", [P, SLOTS, HALF], F32) for h in range(2)]
        by_n2_first = tile("by_n2_first", [P, SLOTS, HALF], F32)
        for t in range(SLOTS):
            times_gy(by_n1[0], n1_l, 0, t)
            times_gy(by_n2_first, n2_l, 0, t)
        times_gy(by_n1[1], n1_l, 1, 0)
        nc.vector.tensor_tensor(z[0][:], by_n1[0][:], by_n2_first[:], ALU.subtract)
        z_side = interleave("z_side0", z[0])
        for t in range(1, SLOTS):
            times_gy(by_n1[1], n1_l, 1, t)
        quantise_z_and_score_b(0, z_side)
        for t in range(SLOTS):
            nc.sync.dma_start(out=b_twin[t][:, columns(0)], in_=b_abs[t][:, columns(0)])
        by_n2_second = tile("by_n2_second", [P, SLOTS, HALF], F32, "z0")
        for t in range(SLOTS):
            times_gy(by_n2_second, n2_l, 1, t)
        for some in (slice(0, SLOTS - 1), slice(SLOTS - 1, SLOTS)):
            nc.vector.tensor_tensor(z[1][:, some, :], by_n1[1][:, some, :], by_n2_second[:, some, :], ALU.subtract)
        z_side = interleave("z_side1", z[1])

        ca_s = deal_bytes("ca_s", gather_bytes("ca_s_raw", ca_l, "gy1"), 1)
        quantise_z_and_score_b(1, z_side)
        ca_w = gather_dealt_words("ca_w", ca_l, "z1")

        a_ps = [psum.tile([P, S], F32, name=f"a_ps{t}", tag=f"y_then_a{t}") for t in range(SLOTS)]
        a_neg, a_twin = slots("a_neg"), slots("a_twin")
        for t in range(SLOTS):
            for h in range(2):
                score(a_ps, ca_w, ca_s, h, t)
            size_of_b(b_twin, 1, t)
            nc.scalar.activation(a_neg[t][:], a_ps[t][:], ACT.Copy, scale=-0.0625)
            nc.sync.dma_start(out=a_twin[t][:], in_=a_neg[t][:])

        inverse = []
        for h in range(2):
            sizes = tile(f"sizes{h}", [P, SLOTS, HALF], F32)
            for t in range(SLOTS):
                nc.vector.tensor_tensor(sizes[:, t, :], looked_up(b_abs[t], n4_l, h), b_twin[t][:, columns(h)], ALU.add)
            root = tile(f"root{h}", [P, SLOTS, HALF], F32)
            nc.scalar.activation(root[:], sizes[:], ACT.Abs_reciprocal_sqrt, bias=one_half[:])
            inverse.append(tile(f"inverse{h}", [P, SLOTS, HALF], F32))
            nc.scalar.activation(inverse[h][:], root[:], ACT.Square)

        numerator = [tile(f"numerator{h}", [P, SLOTS, HALF], F32) for h in range(2)]
        for t in range(SLOTS):
            for h in range(2):
                nc.vector.tensor_tensor(
                    numerator[h][:, t, :], looked_up(a_neg[t], n3_l, h), a_twin[t][:, columns(h)], ALU.subtract
                )

        out_rows = out_0.rearrange("(p t) j -> p t j", t=SLOTS)

        def divide(name, h, lo, hi):
            got = tile(name, [P, SLOTS, hi - lo], F32)
            nc.vector.tensor_tensor(got[:], numerator[h][:, :, lo:hi], inverse[h][:, :, lo:hi], ALU.mult)
            nc.sync.dma_start(out=out_rows[:, :, HALF * h + lo : HALF * h + hi], in_=got[:])
            return got

        out_side = [interleave("out_side0", divide("out_first", 0, 0, HALF)), tile("out_side1", [P, HALF, SLOTS], BF16)]
        quarters = [divide(f"out_quarter{i}", 1, QUARTER * i, QUARTER * (i + 1)) for i in range(2)]
        for i in range(2):
            nc.vector.tensor_copy(
                out_side[1][:, QUARTER * i : QUARTER * (i + 1), :], quarters[i][:].rearrange("p t j -> p j t")
            )

        out_w = tile("out_w", [P, S], I32)
        out_s = tile("out_s", [P, S], U8)
        word_rows = out_1[0].rearrange("p n t -> p (n t)").bitcast(I32)
        for h in range(2):
            quantise(out_w[:, columns(h)], out_s[:, columns(h)], out_side[h])
            nc.sync.dma_start(out=word_rows[:, columns(h)], in_=out_w[:, columns(h)])
        for q in range(4):
            queue = nc.scalar if q % 2 == 0 else nc.sync
            queue.dma_start(
                out=out_2[0, 4 * q : 4 * q + 4, :].bitcast(I32), in_=out_s[32 * q : 32 * q + 4, :].bitcast(I32)
            )
